import numpy as np, ml_dtypes
CORES = [10,34,74,98]
N = 4
TK = 512
def silu(z): return z / (1.0 + np.exp(-z))
def setup_inputs(rng):
    return {"x": rng.standard_normal((N, 128, TK), dtype=np.float32).astype(ml_dtypes.bfloat16), "w1": (rng.standard_normal((N, 128, 128), dtype=np.float32) / 8).astype(ml_dtypes.bfloat16), "w3": (rng.standard_normal((N, 128, 128), dtype=np.float32) / 8).astype(ml_dtypes.bfloat16), "w2": (rng.standard_normal((N, 128, 128), dtype=np.float32) / 8).astype(ml_dtypes.bfloat16)}
def setup_inputs_big(rng):
    d = setup_inputs(rng)
    for k in ("x",): d[k] = (d[k].astype(np.float32) * 1024.0).astype(d[k].dtype)
    return d
def setup_inputs_small(rng):
    d = setup_inputs(rng)
    for k in ("x",): d[k] = (d[k].astype(np.float32) * (1 / 1024.0)).astype(d[k].dtype)
    return d
def setup_inputs_apart(rng):
    d = setup_inputs(rng)
    f = (10.0 ** rng.permutation(np.linspace(-1.5, 1.5, N))).astype(np.float32).reshape(N, 1, 1)
    for k in ("x",): d[k] = (d[k].astype(np.float32) * f).astype(d[k].dtype)
    return d
def reference(x, w1, w3, w2):
    X, W1, W3, W2 = x.astype(np.float64), w1.astype(np.float64), w3.astype(np.float64), w2.astype(np.float64)
    y = np.zeros((N, 128, TK))
    for r in range(N):
        for j in range(N):
            y[r] += W2[j].T @ (silu(W1[j].T @ X[r]) * (W3[j].T @ X[r]))
    return {"y": y.astype(ml_dtypes.bfloat16)}

@@ -1,0 +1,132 @@
+from concourse.mybir import AluOpType, ActivationFunctionType
+
+D = 128
+TK = 512
+C = 128
+NCH = TK // C
+NR = 4
+WC = 3 * D
+NT = NR * NCH
+
+SCRATCH = {
+    "wall": ("sbuf", [D, NR * WC], "bfloat16"),
+    "xs": ("sbuf", [D, TK], "bfloat16"),
+    "s": ("sbuf", [D, NT * C], "float32"),
+    "h": ("sbuf", [D, NT * C], "bfloat16"),
+    "o": ("sbuf", [D, TK], "bfloat16"),
+    "pa0": ("psum", [D, 512], "float32"), "pa1": ("psum", [D, 512], "float32"),
+    "pb0": ("psum", [D, 512], "float32"), "pb1": ("psum", [D, 512], "float32"),
+    "py0": ("psum", [D, 512], "float32"), "py1": ("psum", [D, 512], "float32"),
+    "py2": ("psum", [D, 512], "float32"), "py3": ("psum", [D, 512], "float32"),
+}
+SEMAPHORES = ["ld_w", "ld_x", "sent", "arr1", "arr2", "arr3",
+              "a0", "a1", "b0", "b1", "s0", "s1", "h0", "h1",
+              "y0", "y1", "y2", "y3", "o_lo", "o_hi", "stored"]
+
+
+def _links(topo, a, b):
+    ca, cb = topo.chip(a), topo.chip(b)
+    if ca == cb:
+        return 0
+    return 1 if (topo.mates(ca, cb) or topo.same_plane(ca, cb)) else 2
+
+
+def rank_program(g, core, T, topo):
+    rank = T.rank_of(core)
+    if rank is None:
+        return
+    cores = T.cores
+    n = len(cores)
+    sem = T.sem
+    pe, act, dve, sync = g.tensor, g.scalar, g.vector, g.sync
+
+    offs = sorted(range(1, n), key=lambda k: (max(_links(topo, cores[i], cores[(i + k) % n]) for i in range(n)), k))
+
+    def slot(j, m=None):
+        if m is None:
+            return T.wall[:, j * WC:(j + 1) * WC]
+        return T.wall[:, j * WC + m * D:j * WC + (m + 1) * D]
+
+    hp = D // 2
+    w2c = rank * WC + 2 * D
+    sync.dma_start(slot(rank, 0), T.w1[:]).then_inc(sem.ld_w, 16)
+    act.dma_start(slot(rank, 1), T.w3[:]).then_inc(sem.ld_w, 16)
+    sync.dma_start(T.wall[0:hp, w2c:w2c + D], T.w2[0:hp, :]).then_inc(sem.ld_w, 16)
+    act.dma_start(T.wall[hp:D, w2c:w2c + D], T.w2[hp:D, :]).then_inc(sem.ld_w, 16)
+    sync.dma_start(T.xs[0:hp, :], T.x[0:hp, :]).then_inc(sem.ld_x, 16)
+    act.dma_start(T.xs[hp:D, :], T.x[hp:D, :]).then_inc(sem.ld_x, 16)
+
+    g.wait_ge(sem.ld_w, 64)
+    left = 0
+    eng = []
+    for r, k in enumerate(offs, 1):
+        dst = cores[(rank + k) % n]
+        assert topo.may_write(core, dst)
+        rid, pid, _ = topo.addr(dst)
+        mask = topo.mask(core, dst)
+        g.remote_dma(slot(rank), slot(rank), sem["arr%d" % r], sem.sent, pid, rid, mask)
+        left += bin(mask).count("1")
+        eng.append(bin(topo.mask(cores[(rank - k) % n], core)).count("1"))
+    g.wait_ge(sem.sent, left)
+
+    order = [rank] + [(rank - k) % n for k in offs]
+    PA, PB = [T.pa0, T.pa1], [T.pb0, T.pb1]
+    PY = [T.py0, T.py1, T.py2, T.py3]
+    SA, SB = [sem.a0, sem.a1], [sem.b0, sem.b1]
+    SS, SH = [sem.s0, sem.s1], [sem.h0, sem.h1]
+    SY = [sem.y0, sem.y1, sem.y2, sem.y3]
+
+    def col(buf, t):
+        return buf[:, t * C:(t + 1) * C]
+
+    def y_matmul(t):
+        jj, c = divmod(t, NCH)
+        pe.wait_ge(SH[t % 2], t // 2 + 1)
+        mm = pe.matmul(PY[c][:, 0:C], slot(order[jj], 2), col(T.h, t), jj == 0, jj == n - 1)
+        if jj == n - 1:
+            mm.then_inc(SY[c], 1)
+
+    pe.wait_ge(sem.ld_w, 64)
+    pe.wait_ge(sem.ld_x, 32)
+    pending = None
+    for t in range(NT):
+        jj, c = divmod(t, NCH)
+        if c == 0 and jj > 0:
+            if jj == 1 and pending is not None:
+                y_matmul(pending)
+                pending = None
+            pe.wait_ge(sem["arr%d" % jj], eng[jj - 1])
+        if t >= 2:
+            pe.wait_ge(SS[t % 2], t // 2)
+        pe.matmul(PA[t % 2][:, 0:C], slot(order[jj], 0), col(T.xs, c), True, True).then_inc(SA[t % 2], 1)
+        if t >= 2:
+            pe.wait_ge(SH[t % 2], t // 2)
+        pe.matmul(PB[t % 2][:, 0:C], slot(order[jj], 1), col(T.xs, c), True, True).then_inc(SB[t % 2], 1)
+        if pending is not None:
+            y_matmul(pending)
+        pending = t
+    y_matmul(pending)
+
+    for t in range(NT):
+        act.wait_ge(SA[t % 2], t // 2 + 1)
+        act.activation(col(T.s, t), PA[t % 2][:, 0:C], ActivationFunctionType.Silu).then_inc(SS[t % 2], 1)
+
+    def y_round(c):
+        dve.wait_ge(SY[c], 1)
+        dve.tensor_copy(col(T.o, c), PY[c][:, 0:C]).then_inc(sem.o_lo if c < NCH // 2 else sem.o_hi, 1)
+
+    for t in range(NT):
+        dve.wait_ge(SS[t % 2], t // 2 + 1)
+        dve.wait_ge(SB[t % 2], t // 2 + 1)
+        dve.tensor_tensor(col(T.h, t), col(T.s, t), PB[t % 2][:, 0:C], AluOpType.mult).then_inc(SH[t % 2], 1)
+        c_done = t - (NT - NCH) - 1
+        if c_done >= 0:
+            y_round(c_done)
+    y_round(NCH - 1)
+
+    hk = TK // 2
+    sync.wait_ge(sem.o_lo, NCH // 2)
+    sync.dma_start(T.y[:, 0:hk], T.o[:, 0:hk]).then_inc(sem.stored, 16)
+    sync.wait_ge(sem.o_hi, NCH // 2)
+    sync.dma_start(T.y[:, hk:TK], T.o[:, hk:TK]).then_inc(sem.stored, 16)
+    sync.wait_ge(sem.stored, 32)

@@ -14,14 +14,13 @@ SCRATCH = {
     "s": ("sbuf", [D, NT * C], "float32"),
     "h": ("sbuf", [D, NT * C], "bfloat16"),
     "o": ("sbuf", [D, TK], "bfloat16"),
-    "pa0": ("psum", [D, 512], "float32"), "pa1": ("psum", [D, 512], "float32"),
-    "pb0": ("psum", [D, 512], "float32"), "pb1": ("psum", [D, 512], "float32"),
-    "py0": ("psum", [D, 512], "float32"), "py1": ("psum", [D, 512], "float32"),
-    "py2": ("psum", [D, 512], "float32"), "py3": ("psum", [D, 512], "float32"),
 }
-SEMAPHORES = ["ld_w", "ld_x", "sent", "arr1", "arr2", "arr3",
-              "a0", "a1", "b0", "b1", "s0", "s1", "h0", "h1",
-              "y0", "y1", "y2", "y3", "o_lo", "o_hi", "stored"]
+for _b in range(8):
+    SCRATCH["p%d" % _b] = ("psum", [D, 512], "float32")
+
+SEMAPHORES = (["lw1", "lw3", "lw2", "lx0", "lx1", "sent", "up1", "up2", "up3", "down1", "down2", "down3"]
+              + ["%s%d" % (q, i) for q in "absh" for i in range(4)]
+              + ["y0", "y1", "y2", "y3", "o_lo", "o_hi", "stored"])
 
 
 def _links(topo, a, b):
@@ -42,87 +41,106 @@ def rank_program(g, core, T, topo):
 
     offs = sorted(range(1, n), key=lambda k: (max(_links(topo, cores[i], cores[(i + k) % n]) for i in range(n)), k))
 
-    def slot(j, m=None):
-        if m is None:
-            return T.wall[:, j * WC:(j + 1) * WC]
-        return T.wall[:, j * WC + m * D:j * WC + (m + 1) * D]
+    def slot(j, m, m_end=None):
+        return T.wall[:, j * WC + m * D:j * WC + (m + 1 if m_end is None else m_end) * D]
 
-    hp = D // 2
-    w2c = rank * WC + 2 * D
-    sync.dma_start(slot(rank, 0), T.w1[:]).then_inc(sem.ld_w, 16)
-    act.dma_start(slot(rank, 1), T.w3[:]).then_inc(sem.ld_w, 16)
-    sync.dma_start(T.wall[0:hp, w2c:w2c + D], T.w2[0:hp, :]).then_inc(sem.ld_w, 16)
-    act.dma_start(T.wall[hp:D, w2c:w2c + D], T.w2[hp:D, :]).then_inc(sem.ld_w, 16)
-    sync.dma_start(T.xs[0:hp, :], T.x[0:hp, :]).then_inc(sem.ld_x, 16)
-    act.dma_start(T.xs[hp:D, :], T.x[hp:D, :]).then_inc(sem.ld_x, 16)
+    sync.dma_start(slot(rank, 0), T.w1[:]).then_inc(sem.lw1, 16)
+    act.dma_start(slot(rank, 1), T.w3[:]).then_inc(sem.lw3, 16)
+    sync.dma_start(T.xs[:, 0:C], T.x[:, 0:C]).then_inc(sem.lx0, 16)
+    act.dma_start(slot(rank, 2), T.w2[:]).then_inc(sem.lw2, 16)
+    sync.dma_start(T.xs[:, C:TK], T.x[:, C:TK]).then_inc(sem.lx1, 16)
 
-    g.wait_ge(sem.ld_w, 64)
+    g.wait_ge(sem.lw1, 16)
+    g.wait_ge(sem.lw3, 16)
     left = 0
-    eng = []
+    eng = [0]
     for r, k in enumerate(offs, 1):
         dst = cores[(rank + k) % n]
         assert topo.may_write(core, dst)
         rid, pid, _ = topo.addr(dst)
         mask = topo.mask(core, dst)
-        g.remote_dma(slot(rank), slot(rank), sem["arr%d" % r], sem.sent, pid, rid, mask)
-        left += bin(mask).count("1")
+        g.remote_dma(slot(rank, 0, 2), slot(rank, 0, 2), sem["up%d" % r], sem.sent, pid, rid, mask)
+        if r == 1:
+            g.wait_ge(sem.lw2, 16)
+        g.remote_dma(slot(rank, 2), slot(rank, 2), sem["down%d" % r], sem.sent, pid, rid, mask)
+        left += 2 * bin(mask).count("1")
         eng.append(bin(topo.mask(cores[(rank - k) % n], core)).count("1"))
     g.wait_ge(sem.sent, left)
 
     order = [rank] + [(rank - k) % n for k in offs]
-    PA, PB = [T.pa0, T.pa1], [T.pb0, T.pb1]
-    PY = [T.py0, T.py1, T.py2, T.py3]
-    SA, SB = [sem.a0, sem.a1], [sem.b0, sem.b1]
-    SS, SH = [sem.s0, sem.s1], [sem.h0, sem.h1]
-    SY = [sem.y0, sem.y1, sem.y2, sem.y3]
+
+    def bank(b):
+        return T["p%d" % b][:, 0:C]
+
+    def bank_a(t):
+        return bank(2 * t if t < NCH else 4 + 2 * (t % 2))
+
+    def bank_b(t):
+        return bank(2 * t + 1 if t < NCH else 5 + 2 * (t % 2))
+
+    def cnt(q, t):
+        return sem["%s%d" % (q, t % 4)], t // 4 + 1
 
     def col(buf, t):
         return buf[:, t * C:(t + 1) * C]
 
-    def y_matmul(t):
-        jj, c = divmod(t, NCH)
-        pe.wait_ge(SH[t % 2], t // 2 + 1)
-        mm = pe.matmul(PY[c][:, 0:C], slot(order[jj], 2), col(T.h, t), jj == 0, jj == n - 1)
-        if jj == n - 1:
-            mm.then_inc(SY[c], 1)
-
-    pe.wait_ge(sem.ld_w, 64)
-    pe.wait_ge(sem.ld_x, 32)
-    pending = None
-    for t in range(NT):
+    def ab_matmul(t):
         jj, c = divmod(t, NCH)
         if c == 0 and jj > 0:
-            if jj == 1 and pending is not None:
-                y_matmul(pending)
-                pending = None
-            pe.wait_ge(sem["arr%d" % jj], eng[jj - 1])
-        if t >= 2:
-            pe.wait_ge(SS[t % 2], t // 2)
-        pe.matmul(PA[t % 2][:, 0:C], slot(order[jj], 0), col(T.xs, c), True, True).then_inc(SA[t % 2], 1)
-        if t >= 2:
-            pe.wait_ge(SH[t % 2], t // 2)
-        pe.matmul(PB[t % 2][:, 0:C], slot(order[jj], 1), col(T.xs, c), True, True).then_inc(SB[t % 2], 1)
-        if pending is not None:
-            y_matmul(pending)
-        pending = t
-    y_matmul(pending)
+            pe.wait_ge(sem["up%d" % jj], eng[jj])
+        if t >= NCH + 2:
+            pe.wait_ge(*cnt("s", t - 2))
+        pe.matmul(bank_a(t), slot(order[jj], 0), col(T.xs, c), True, True).then_inc(cnt("a", t)[0], 1)
+        if t >= NCH + 2:
+            pe.wait_ge(*cnt("h", t - 2))
+        pe.matmul(bank_b(t), slot(order[jj], 1), col(T.xs, c), True, True).then_inc(cnt("b", t)[0], 1)
+
+    def y_matmul(t):
+        jj, c = divmod(t, NCH)
+        if c == 0 and jj > 0:
+            pe.wait_ge(sem["down%d" % jj], eng[jj])
+        pe.wait_ge(*cnt("h", t))
+        mm = pe.matmul(bank(c), slot(order[jj], 2), col(T.h, t), jj == 0, jj == n - 1)
+        if jj == n - 1:
+            mm.then_inc(sem["y%d" % c], 1)
+
+    pe.wait_ge(sem.lw1, 16)
+    pe.wait_ge(sem.lx0, 16)
+    pe.matmul(bank_a(0), slot(rank, 0), col(T.xs, 0), True, True).then_inc(cnt("a", 0)[0], 1)
+    pe.wait_ge(sem.lw3, 16)
+    pe.matmul(bank_b(0), slot(rank, 1), col(T.xs, 0), True, True).then_inc(cnt("b", 0)[0], 1)
+    pe.wait_ge(sem.lx1, 16)
+    for t in range(1, NCH):
+        ab_matmul(t)
+    pe.wait_ge(sem.lw2, 16)
+    for t in range(NCH):
+        y_matmul(t)
+    for jj in range(1, n - 1):
+        for t in range(jj * NCH, (jj + 1) * NCH):
+            ab_matmul(t)
+        for t in range(jj * NCH, (jj + 1) * NCH):
+            y_matmul(t)
+    z = NT - NCH
+    for t in (z, z + 1, z + 2):
+        ab_matmul(t)
+    y_matmul(z)
+    y_matmul(z + 1)
+    ab_matmul(z + 3)
+    y_matmul(z + 2)
+    y_matmul(z + 3)
+    rounds_after = {z + 2: (0, 1), z + 3: (2, 3)}
 
     for t in range(NT):
-        act.wait_ge(SA[t % 2], t // 2 + 1)
-        act.activation(col(T.s, t), PA[t % 2][:, 0:C], ActivationFunctionType.Silu).then_inc(SS[t % 2], 1)
-
-    def y_round(c):
-        dve.wait_ge(SY[c], 1)
-        dve.tensor_copy(col(T.o, c), PY[c][:, 0:C]).then_inc(sem.o_lo if c < NCH // 2 else sem.o_hi, 1)
+        act.wait_ge(*cnt("a", t))
+        act.activation(col(T.s, t), bank_a(t), ActivationFunctionType.Silu).then_inc(cnt("s", t)[0], 1)
 
     for t in range(NT):
-        dve.wait_ge(SS[t % 2], t // 2 + 1)
-        dve.wait_ge(SB[t % 2], t // 2 + 1)
-        dve.tensor_tensor(col(T.h, t), col(T.s, t), PB[t % 2][:, 0:C], AluOpType.mult).then_inc(SH[t % 2], 1)
-        c_done = t - (NT - NCH) - 1
-        if c_done >= 0:
-            y_round(c_done)
-    y_round(NCH - 1)
+        dve.wait_ge(*cnt("s", t))
+        dve.wait_ge(*cnt("b", t))
+        dve.tensor_tensor(col(T.h, t), col(T.s, t), bank_b(t), AluOpType.mult).then_inc(cnt("h", t)[0], 1)
+        for c in rounds_after.get(t, ()):
+            dve.wait_ge(sem["y%d" % c], 1)
+            dve.tensor_copy(col(T.o, c), bank(c)).then_inc(sem.o_lo if c < NCH // 2 else sem.o_hi, 1)
 
     hk = TK // 2
     sync.wait_ge(sem.o_lo, NCH // 2)

@@ -7,6 +7,7 @@ NCH = TK // C
 NR = 4
 WC = 3 * D
 NT = NR * NCH
+NCORES = 112
 
 SCRATCH = {
     "wall": ("sbuf", [D, NR * WC], "bfloat16"),
@@ -18,7 +19,8 @@ SCRATCH = {
 for _b in range(8):
     SCRATCH["p%d" % _b] = ("psum", [D, 512], "float32")
 
-SEMAPHORES = (["lw1", "lw3", "lw2", "lx0", "lx1", "sent", "up1", "up2", "up3", "down1", "down2", "down3"]
+SEMAPHORES = (["lw1", "lw3", "lw2", "lx0", "lx1", "sent", "up1", "up2", "up3", "down1", "down2", "down3",
+               "qup", "qdown"]
               + ["%s%d" % (q, i) for q in "absh" for i in range(4)]
               + ["y0", "y1", "y2", "y3", "o_lo", "o_hi", "stored"])
 
@@ -30,19 +32,48 @@ def _links(topo, a, b):
     return 1 if (topo.mates(ca, cb) or topo.same_plane(ca, cb)) else 2
 
 
+def _ones(mask):
+    return bin(mask).count("1")
+
+
 def rank_program(g, core, T, topo):
-    rank = T.rank_of(core)
-    if rank is None:
-        return
     cores = T.cores
     n = len(cores)
     sem = T.sem
-    pe, act, dve, sync = g.tensor, g.scalar, g.vector, g.sync
 
     offs = sorted(range(1, n), key=lambda k: (max(_links(topo, cores[i], cores[(i + k) % n]) for i in range(n)), k))
+    k_help, k_own = offs[0], offs[1:]
+
+    def helper_of(i):
+        me, dst = cores[i], cores[(i + k_help) % n]
+        return [c for c in range(NCORES) if c not in cores and topo.chip(c) == topo.chip(me)
+                and topo.die(c) == topo.die(me) and topo.may_write(c, dst)][0]
 
     def slot(j, m, m_end=None):
         return T.wall[:, j * WC + m * D:j * WC + (m + 1 if m_end is None else m_end) * D]
+
+    def feed_mask(i):
+        on = topo.mask(cores[i], helper_of(i))
+        free = on & ~topo.mask(cores[i], cores[(i + k_own[0]) % n])
+        return free if free else on
+
+    for i in range(n):
+        if core == helper_of(i):
+            dst = cores[(i + k_help) % n]
+            rid, pid, _ = topo.addr(dst)
+            mask = topo.mask(core, dst)
+            fed = _ones(feed_mask(i))
+            g.wait_ge(sem.qup, fed)
+            g.remote_dma(slot(i, 0, 2), slot(i, 0, 2), sem.up3, sem.sent, pid, rid, mask)
+            g.wait_ge(sem.qdown, fed)
+            g.remote_dma(slot(i, 2), slot(i, 2), sem.down3, sem.sent, pid, rid, mask)
+            g.wait_ge(sem.sent, 2 * _ones(mask))
+            return
+
+    rank = T.rank_of(core)
+    if rank is None:
+        return
+    pe, act, dve, sync = g.tensor, g.scalar, g.vector, g.sync
 
     sync.dma_start(slot(rank, 0), T.w1[:]).then_inc(sem.lw1, 16)
     act.dma_start(slot(rank, 1), T.w3[:]).then_inc(sem.lw3, 16)
@@ -50,24 +81,29 @@ def rank_program(g, core, T, topo):
     act.dma_start(slot(rank, 2), T.w2[:]).then_inc(sem.lw2, 16)
     sync.dma_start(T.xs[:, C:TK], T.x[:, C:TK]).then_inc(sem.lx1, 16)
 
+    hrid, hpid, _ = topo.addr(helper_of(rank))
+    hmask = feed_mask(rank)
+    left = 0
     g.wait_ge(sem.lw1, 16)
     g.wait_ge(sem.lw3, 16)
-    left = 0
-    eng = [0]
-    for r, k in enumerate(offs, 1):
+    for r, k in enumerate(k_own, 1):
         dst = cores[(rank + k) % n]
         assert topo.may_write(core, dst)
         rid, pid, _ = topo.addr(dst)
         mask = topo.mask(core, dst)
         g.remote_dma(slot(rank, 0, 2), slot(rank, 0, 2), sem["up%d" % r], sem.sent, pid, rid, mask)
         if r == 1:
+            g.remote_dma(slot(rank, 0, 2), slot(rank, 0, 2), sem.qup, sem.sent, hpid, hrid, hmask)
             g.wait_ge(sem.lw2, 16)
         g.remote_dma(slot(rank, 2), slot(rank, 2), sem["down%d" % r], sem.sent, pid, rid, mask)
-        left += 2 * bin(mask).count("1")
-        eng.append(bin(topo.mask(cores[(rank - k) % n], core)).count("1"))
+        if r == 1:
+            g.remote_dma(slot(rank, 2), slot(rank, 2), sem.qdown, sem.sent, hpid, hrid, hmask)
+            left += 2 * _ones(hmask)
+        left += 2 * _ones(mask)
     g.wait_ge(sem.sent, left)
 
-    order = [rank] + [(rank - k) % n for k in offs]
+    order = [rank] + [(rank - k) % n for k in k_own] + [(rank - k_help) % n]
+    eng = [0] + [_ones(topo.mask(cores[j], core)) for j in order[1:n - 1]] + [_ones(topo.mask(helper_of(order[-1]), core))]
 
     def bank(b):
         return T["p%d" % b][:, 0:C]
@@ -115,20 +151,14 @@ def rank_program(g, core, T, topo):
     pe.wait_ge(sem.lw2, 16)
     for t in range(NCH):
         y_matmul(t)
-    for jj in range(1, n - 1):
-        for t in range(jj * NCH, (jj + 1) * NCH):
-            ab_matmul(t)
-        for t in range(jj * NCH, (jj + 1) * NCH):
-            y_matmul(t)
-    z = NT - NCH
-    for t in (z, z + 1, z + 2):
+    for t in range(NCH, 2 * NCH):
         ab_matmul(t)
-    y_matmul(z)
-    y_matmul(z + 1)
-    ab_matmul(z + 3)
-    y_matmul(z + 2)
-    y_matmul(z + 3)
-    rounds_after = {z + 2: (0, 1), z + 3: (2, 3)}
+    for t in range(NCH, 2 * NCH):
+        y_matmul(t)
+    for t in range(2 * NCH, NT):
+        ab_matmul(t)
+    for t in range(2 * NCH, NT):
+        y_matmul(t)
 
     for t in range(NT):
         act.wait_ge(*cnt("a", t))
@@ -138,9 +168,9 @@ def rank_program(g, core, T, topo):
         dve.wait_ge(*cnt("s", t))
         dve.wait_ge(*cnt("b", t))
         dve.tensor_tensor(col(T.h, t), col(T.s, t), bank_b(t), AluOpType.mult).then_inc(cnt("h", t)[0], 1)
-        for c in rounds_after.get(t, ()):
-            dve.wait_ge(sem["y%d" % c], 1)
-            dve.tensor_copy(col(T.o, c), bank(c)).then_inc(sem.o_lo if c < NCH // 2 else sem.o_hi, 1)
+    for c in range(NCH):
+        dve.wait_ge(sem["y%d" % c], 1)
+        dve.tensor_copy(col(T.o, c), bank(c)).then_inc(sem.o_lo if c < NCH // 2 else sem.o_hi, 1)
 
     hk = TK // 2
     sync.wait_ge(sem.o_lo, NCH // 2)

@@ -1,12 +1,14 @@
+from concourse.bass import DstId, RemoteDMATransfer
 from concourse.mybir import AluOpType, ActivationFunctionType
 
 D = 128
 TK = 512
-C = 128
+C = 256
 NCH = TK // C
 NR = 4
 WC = 3 * D
 NT = NR * NCH
+NPAIR = 3
 NCORES = 112
 
 SCRATCH = {
@@ -21,8 +23,8 @@ for _b in range(8):
 
 SEMAPHORES = (["lw1", "lw3", "lw2", "lx0", "lx1", "sent", "up1", "up2", "up3", "down1", "down2", "down3",
                "qup", "qdown"]
-              + ["%s%d" % (q, i) for q in "absh" for i in range(4)]
-              + ["y0", "y1", "y2", "y3", "o_lo", "o_hi", "stored"])
+              + ["%s%d" % (q, i) for q in "absh" for i in range(NT)]
+              + ["y0", "y1", "o0", "o1", "st0", "st1"])
 
 
 def _links(topo, a, b):
@@ -34,6 +36,12 @@ def _links(topo, a, b):
 
 def _ones(mask):
     return bin(mask).count("1")
+
+
+def _halves(mask):
+    bits = [b for b in range(mask.bit_length()) if mask >> b & 1]
+    h = len(bits) // 2
+    return sum(1 << b for b in bits[:h]), sum(1 << b for b in bits[h:])
 
 
 def rank_program(g, core, T, topo):
@@ -54,8 +62,15 @@ def rank_program(g, core, T, topo):
 
     def feed_mask(i):
         on = topo.mask(cores[i], helper_of(i))
-        free = on & ~topo.mask(cores[i], cores[(i + k_own[0]) % n])
-        return free if free else on
+        return on & ~topo.mask(cores[i], cores[(i + k_own[0]) % n])
+
+    def off_mask(i):
+        return topo.mask(cores[i], cores[(i + k_own[0]) % n]) & topo.mask(cores[i], cores[(i + k_own[1]) % n])
+
+    def xfer(dst, ap, mask, remote_sem):
+        rid, pid, _ = topo.addr(dst)
+        return RemoteDMATransfer(dst_ids=[DstId(rid=rid, pnc=pid)], dma_engine_mask=mask, remote_sem=remote_sem,
+                                 src=ap, dst=ap)
 
     for i in range(n):
         if core == helper_of(i):
@@ -81,41 +96,37 @@ def rank_program(g, core, T, topo):
     act.dma_start(slot(rank, 2), T.w2[:]).then_inc(sem.lw2, 16)
     sync.dma_start(T.xs[:, C:TK], T.x[:, C:TK]).then_inc(sem.lx1, 16)
 
-    hrid, hpid, _ = topo.addr(helper_of(rank))
-    hmask = feed_mask(rank)
-    left = 0
+    dst1, dst2 = cores[(rank + k_own[0]) % n], cores[(rank + k_own[1]) % n]
+    assert topo.may_write(core, dst1) and topo.may_write(core, dst2)
+    helper = helper_of(rank)
+    omask, hmask = off_mask(rank), feed_mask(rank)
+    lo, hi = _halves(omask)
+    up, down = slot(rank, 0, 2), slot(rank, 2)
     g.wait_ge(sem.lw1, 16)
     g.wait_ge(sem.lw3, 16)
-    for r, k in enumerate(k_own, 1):
-        dst = cores[(rank + k) % n]
-        assert topo.may_write(core, dst)
-        rid, pid, _ = topo.addr(dst)
-        mask = topo.mask(core, dst)
-        g.remote_dma(slot(rank, 0, 2), slot(rank, 0, 2), sem["up%d" % r], sem.sent, pid, rid, mask)
-        if r == 1:
-            g.remote_dma(slot(rank, 0, 2), slot(rank, 0, 2), sem.qup, sem.sent, hpid, hrid, hmask)
-            g.wait_ge(sem.lw2, 16)
-        g.remote_dma(slot(rank, 2), slot(rank, 2), sem["down%d" % r], sem.sent, pid, rid, mask)
-        if r == 1:
-            g.remote_dma(slot(rank, 2), slot(rank, 2), sem.qdown, sem.sent, hpid, hrid, hmask)
-            left += 2 * _ones(hmask)
-        left += 2 * _ones(mask)
-    g.wait_ge(sem.sent, left)
+    g.remote_dma_fused([xfer(dst1, up, omask, sem.up1)], local_sem=sem.sent)
+    g.remote_dma_fused([xfer(dst2, up, omask, sem.up2), xfer(helper, up, hmask, sem.qup)], local_sem=sem.sent)
+    g.wait_ge(sem.lw2, 16)
+    g.remote_dma_fused([xfer(dst1, down, lo, sem.down1), xfer(dst2, down, hi, sem.down2),
+                        xfer(helper, down, hmask, sem.qdown)], local_sem=sem.sent)
+    g.wait_ge(sem.sent, 3 * _ones(omask) + 2 * _ones(hmask))
 
     order = [rank] + [(rank - k) % n for k in k_own] + [(rank - k_help) % n]
-    eng = [0] + [_ones(topo.mask(cores[j], core)) for j in order[1:n - 1]] + [_ones(topo.mask(helper_of(order[-1]), core))]
+    help_eng = _ones(topo.mask(helper_of(order[-1]), core))
+    eng_up = [0, _ones(off_mask(order[1])), _ones(off_mask(order[2])), help_eng]
+    eng_down = [0, _ones(_halves(off_mask(order[1]))[0]), _ones(_halves(off_mask(order[2]))[1]), help_eng]
 
     def bank(b):
         return T["p%d" % b][:, 0:C]
 
     def bank_a(t):
-        return bank(2 * t if t < NCH else 4 + 2 * (t % 2))
+        return bank(NCH + 2 * (t % NPAIR))
 
     def bank_b(t):
-        return bank(2 * t + 1 if t < NCH else 5 + 2 * (t % 2))
+        return bank(NCH + 2 * (t % NPAIR) + 1)
 
-    def cnt(q, t):
-        return sem["%s%d" % (q, t % 4)], t // 4 + 1
+    def done(q, t):
+        return sem["%s%d" % (q, t)]
 
     def col(buf, t):
         return buf[:, t * C:(t + 1) * C]
@@ -123,58 +134,58 @@ def rank_program(g, core, T, topo):
     def ab_matmul(t):
         jj, c = divmod(t, NCH)
         if c == 0 and jj > 0:
-            pe.wait_ge(sem["up%d" % jj], eng[jj])
-        if t >= NCH + 2:
-            pe.wait_ge(*cnt("s", t - 2))
-        pe.matmul(bank_a(t), slot(order[jj], 0), col(T.xs, c), True, True).then_inc(cnt("a", t)[0], 1)
-        if t >= NCH + 2:
-            pe.wait_ge(*cnt("h", t - 2))
-        pe.matmul(bank_b(t), slot(order[jj], 1), col(T.xs, c), True, True).then_inc(cnt("b", t)[0], 1)
+            pe.wait_ge(sem["up%d" % jj], eng_up[jj])
+        if t >= NPAIR:
+            pe.wait_ge(done("s", t - NPAIR), 1)
+        pe.matmul(bank_a(t), slot(order[jj], 0), col(T.xs, c), True, True).then_inc(done("a", t), 1)
+        if t >= NPAIR:
+            pe.wait_ge(done("h", t - NPAIR), 1)
+        pe.matmul(bank_b(t), slot(order[jj], 1), col(T.xs, c), True, True).then_inc(done("b", t), 1)
 
     def y_matmul(t):
         jj, c = divmod(t, NCH)
         if c == 0 and jj > 0:
-            pe.wait_ge(sem["down%d" % jj], eng[jj])
-        pe.wait_ge(*cnt("h", t))
+            pe.wait_ge(sem["down%d" % jj], eng_down[jj])
+        pe.wait_ge(done("h", t), 1)
         mm = pe.matmul(bank(c), slot(order[jj], 2), col(T.h, t), jj == 0, jj == n - 1)
         if jj == n - 1:
             mm.then_inc(sem["y%d" % c], 1)
 
     pe.wait_ge(sem.lw1, 16)
     pe.wait_ge(sem.lx0, 16)
-    pe.matmul(bank_a(0), slot(rank, 0), col(T.xs, 0), True, True).then_inc(cnt("a", 0)[0], 1)
+    pe.matmul(bank_a(0), slot(rank, 0), col(T.xs, 0), True, True).then_inc(done("a", 0), 1)
     pe.wait_ge(sem.lw3, 16)
-    pe.matmul(bank_b(0), slot(rank, 1), col(T.xs, 0), True, True).then_inc(cnt("b", 0)[0], 1)
+    pe.matmul(bank_b(0), slot(rank, 1), col(T.xs, 0), True, True).then_inc(done("b", 0), 1)
     pe.wait_ge(sem.lx1, 16)
     for t in range(1, NCH):
         ab_matmul(t)
     pe.wait_ge(sem.lw2, 16)
     for t in range(NCH):
         y_matmul(t)
-    for t in range(NCH, 2 * NCH):
+    for t in range(NCH, 3 * NCH):
         ab_matmul(t)
     for t in range(NCH, 2 * NCH):
         y_matmul(t)
-    for t in range(2 * NCH, NT):
+    for t in range(3 * NCH, NT):
         ab_matmul(t)
     for t in range(2 * NCH, NT):
         y_matmul(t)
 
     for t in range(NT):
-        act.wait_ge(*cnt("a", t))
-        act.activation(col(T.s, t), bank_a(t), ActivationFunctionType.Silu).then_inc(cnt("s", t)[0], 1)
+        act.wait_ge(done("a", t), 1)
+        act.activation(col(T.s, t), bank_a(t), ActivationFunctionType.Silu).then_inc(done("s", t), 1)
 
     for t in range(NT):
-        dve.wait_ge(*cnt("s", t))
-        dve.wait_ge(*cnt("b", t))
-        dve.tensor_tensor(col(T.h, t), col(T.s, t), bank_b(t), AluOpType.mult).then_inc(cnt("h", t)[0], 1)
+        dve.wait_ge(done("s", t), 1)
+        dve.wait_ge(done("b", t), 1)
+        dve.tensor_tensor(col(T.h, t), col(T.s, t), bank_b(t), AluOpType.mult).then_inc(done("h", t), 1)
     for c in range(NCH):
         dve.wait_ge(sem["y%d" % c], 1)
-        dve.tensor_copy(col(T.o, c), bank(c)).then_inc(sem.o_lo if c < NCH // 2 else sem.o_hi, 1)
+        dve.tensor_copy(col(T.o, c), bank(c)).then_inc(sem["o%d" % c], 1)
 
-    hk = TK // 2
-    sync.wait_ge(sem.o_lo, NCH // 2)
-    sync.dma_start(T.y[:, 0:hk], T.o[:, 0:hk]).then_inc(sem.stored, 16)
-    sync.wait_ge(sem.o_hi, NCH // 2)
-    sync.dma_start(T.y[:, hk:TK], T.o[:, hk:TK]).then_inc(sem.stored, 16)
-    sync.wait_ge(sem.stored, 32)
+    sync.wait_ge(sem.o0, 1)
+    sync.dma_start(col(T.y, 0), col(T.o, 0)).then_inc(sem.st0, 16)
+    act.wait_ge(sem.o1, 1)
+    act.dma_start(col(T.y, 1), col(T.o, 1)).then_inc(sem.st1, 16)
+    sync.wait_ge(sem.st0, 16)
+    act.wait_ge(sem.st1, 16)

@@ -1,15 +1,17 @@
-from concourse.bass import DstId, RemoteDMATransfer
 from concourse.mybir import AluOpType, ActivationFunctionType
 
 D = 128
 TK = 512
 C = 256
+Q = C // 2
 NCH = TK // C
 NR = 4
 WC = 3 * D
 NT = NR * NCH
-NPAIR = 3
 NCORES = 112
+PIECES = [(0, C), (C, Q), (C + Q, Q)]
+NI = 8 - len(PIECES)
+OWN_Y_AFTER = 3
 
 SCRATCH = {
     "wall": ("sbuf", [D, NR * WC], "bfloat16"),
@@ -21,10 +23,9 @@ SCRATCH = {
 for _b in range(8):
     SCRATCH["p%d" % _b] = ("psum", [D, 512], "float32")
 
-SEMAPHORES = (["lw1", "lw3", "lw2", "lx0", "lx1", "sent", "up1", "up2", "up3", "down1", "down2", "down3",
-               "qup", "qdown"]
+SEMAPHORES = (["lw1", "lw3", "lw2", "lx0", "lx1", "sent", "up1", "up2", "up3", "down1", "down2", "down3", "qdown"]
               + ["%s%d" % (q, i) for q in "absh" for i in range(NT)]
-              + ["y0", "y1", "o0", "o1", "st0", "st1"])
+              + ["%s%d" % (q, p) for q in ("y", "o", "st") for p in range(len(PIECES))])
 
 
 def _links(topo, a, b):
@@ -38,19 +39,13 @@ def _ones(mask):
     return bin(mask).count("1")
 
 
-def _halves(mask):
-    bits = [b for b in range(mask.bit_length()) if mask >> b & 1]
-    h = len(bits) // 2
-    return sum(1 << b for b in bits[:h]), sum(1 << b for b in bits[h:])
-
-
 def rank_program(g, core, T, topo):
     cores = T.cores
     n = len(cores)
     sem = T.sem
 
     offs = sorted(range(1, n), key=lambda k: (max(_links(topo, cores[i], cores[(i + k) % n]) for i in range(n)), k))
-    k_help, k_own = offs[0], offs[1:]
+    k_help = offs[-1]
 
     def helper_of(i):
         me, dst = cores[i], cores[(i + k_help) % n]
@@ -62,27 +57,20 @@ def rank_program(g, core, T, topo):
 
     def feed_mask(i):
         on = topo.mask(cores[i], helper_of(i))
-        return on & ~topo.mask(cores[i], cores[(i + k_own[0]) % n])
+        for k in offs:
+            on &= ~topo.mask(cores[i], cores[(i + k) % n])
+        return on
 
-    def off_mask(i):
-        return topo.mask(cores[i], cores[(i + k_own[0]) % n]) & topo.mask(cores[i], cores[(i + k_own[1]) % n])
-
-    def xfer(dst, ap, mask, remote_sem):
+    def write(dst, ap, mask, remote_sem):
         rid, pid, _ = topo.addr(dst)
-        return RemoteDMATransfer(dst_ids=[DstId(rid=rid, pnc=pid)], dma_engine_mask=mask, remote_sem=remote_sem,
-                                 src=ap, dst=ap)
+        g.remote_dma(ap, ap, remote_sem, sem.sent, pid, rid, mask)
+        return _ones(mask)
 
     for i in range(n):
         if core == helper_of(i):
             dst = cores[(i + k_help) % n]
-            rid, pid, _ = topo.addr(dst)
-            mask = topo.mask(core, dst)
-            fed = _ones(feed_mask(i))
-            g.wait_ge(sem.qup, fed)
-            g.remote_dma(slot(i, 0, 2), slot(i, 0, 2), sem.up3, sem.sent, pid, rid, mask)
-            g.wait_ge(sem.qdown, fed)
-            g.remote_dma(slot(i, 2), slot(i, 2), sem.down3, sem.sent, pid, rid, mask)
-            g.wait_ge(sem.sent, 2 * _ones(mask))
+            g.wait_ge(sem.qdown, _ones(feed_mask(i)))
+            g.wait_ge(sem.sent, write(dst, slot(i, 2), topo.mask(core, dst), sem.down3))
             return
 
     rank = T.rank_of(core)
@@ -96,34 +84,33 @@ def rank_program(g, core, T, topo):
     act.dma_start(slot(rank, 2), T.w2[:]).then_inc(sem.lw2, 16)
     sync.dma_start(T.xs[:, C:TK], T.x[:, C:TK]).then_inc(sem.lx1, 16)
 
-    dst1, dst2 = cores[(rank + k_own[0]) % n], cores[(rank + k_own[1]) % n]
-    assert topo.may_write(core, dst1) and topo.may_write(core, dst2)
-    helper = helper_of(rank)
-    omask, hmask = off_mask(rank), feed_mask(rank)
-    lo, hi = _halves(omask)
+    dsts = [cores[(rank + k) % n] for k in offs]
+    assert all(topo.may_write(core, d) for d in dsts)
     up, down = slot(rank, 0, 2), slot(rank, 2)
     g.wait_ge(sem.lw1, 16)
     g.wait_ge(sem.lw3, 16)
-    g.remote_dma_fused([xfer(dst1, up, omask, sem.up1)], local_sem=sem.sent)
-    g.remote_dma_fused([xfer(dst2, up, omask, sem.up2), xfer(helper, up, hmask, sem.qup)], local_sem=sem.sent)
+    left = write(dsts[0], up, topo.mask(core, dsts[0]), sem.up1)
     g.wait_ge(sem.lw2, 16)
-    g.remote_dma_fused([xfer(dst1, down, lo, sem.down1), xfer(dst2, down, hi, sem.down2),
-                        xfer(helper, down, hmask, sem.qdown)], local_sem=sem.sent)
-    g.wait_ge(sem.sent, 3 * _ones(omask) + 2 * _ones(hmask))
+    left += write(helper_of(rank), down, feed_mask(rank), sem.qdown)
+    left += write(dsts[1], up, topo.mask(core, dsts[1]), sem.up2)
+    left += write(dsts[2], up, topo.mask(core, dsts[2]), sem.up3)
+    left += write(dsts[0], down, topo.mask(core, dsts[0]), sem.down1)
+    left += write(dsts[1], down, topo.mask(core, dsts[1]), sem.down2)
+    g.wait_ge(sem.sent, left)
 
-    order = [rank] + [(rank - k) % n for k in k_own] + [(rank - k_help) % n]
-    help_eng = _ones(topo.mask(helper_of(order[-1]), core))
-    eng_up = [0, _ones(off_mask(order[1])), _ones(off_mask(order[2])), help_eng]
-    eng_down = [0, _ones(_halves(off_mask(order[1]))[0]), _ones(_halves(off_mask(order[2]))[1]), help_eng]
-
-    def bank(b):
-        return T["p%d" % b][:, 0:C]
+    order = [rank] + [(rank - k) % n for k in offs]
+    eng_up = [0] + [_ones(topo.mask(cores[j], core)) for j in order[1:]]
+    eng_down = eng_up[:n - 1] + [_ones(topo.mask(helper_of(order[-1]), core))]
+    np_ = len(PIECES)
 
     def bank_a(t):
-        return bank(NCH + 2 * (t % NPAIR))
+        return T["p%d" % (np_ + t % NI)][:, 0:C]
 
     def bank_b(t):
-        return bank(NCH + 2 * (t % NPAIR) + 1)
+        return T["p%d" % (np_ + t % NI)][:, C:2 * C]
+
+    def bank_y(p):
+        return T["p%d" % p][:, 0:PIECES[p][1]]
 
     def done(q, t):
         return sem["%s%d" % (q, t)]
@@ -135,11 +122,10 @@ def rank_program(g, core, T, topo):
         jj, c = divmod(t, NCH)
         if c == 0 and jj > 0:
             pe.wait_ge(sem["up%d" % jj], eng_up[jj])
-        if t >= NPAIR:
-            pe.wait_ge(done("s", t - NPAIR), 1)
+        if t >= NI:
+            pe.wait_ge(done("s", t - NI), 1)
+            pe.wait_ge(done("h", t - NI), 1)
         pe.matmul(bank_a(t), slot(order[jj], 0), col(T.xs, c), True, True).then_inc(done("a", t), 1)
-        if t >= NPAIR:
-            pe.wait_ge(done("h", t - NPAIR), 1)
         pe.matmul(bank_b(t), slot(order[jj], 1), col(T.xs, c), True, True).then_inc(done("b", t), 1)
 
     def y_matmul(t):
@@ -147,45 +133,46 @@ def rank_program(g, core, T, topo):
         if c == 0 and jj > 0:
             pe.wait_ge(sem["down%d" % jj], eng_down[jj])
         pe.wait_ge(done("h", t), 1)
-        mm = pe.matmul(bank(c), slot(order[jj], 2), col(T.h, t), jj == 0, jj == n - 1)
-        if jj == n - 1:
-            mm.then_inc(sem["y%d" % c], 1)
+        for p, (first, width) in enumerate(PIECES):
+            if first // C != c:
+                continue
+            lo = t * C + first - c * C
+            mm = pe.matmul(bank_y(p), slot(order[jj], 2), T.h[:, lo:lo + width], jj == 0, jj == n - 1)
+            if jj == n - 1:
+                mm.then_inc(sem["y%d" % p], 1)
 
     pe.wait_ge(sem.lw1, 16)
-    pe.wait_ge(sem.lx0, 16)
-    pe.matmul(bank_a(0), slot(rank, 0), col(T.xs, 0), True, True).then_inc(done("a", 0), 1)
     pe.wait_ge(sem.lw3, 16)
-    pe.matmul(bank_b(0), slot(rank, 1), col(T.xs, 0), True, True).then_inc(done("b", 0), 1)
+    pe.wait_ge(sem.lx0, 16)
+    ab_matmul(0)
     pe.wait_ge(sem.lx1, 16)
-    for t in range(1, NCH):
+    ab_matmul(1)
+    for t in range(NCH, NCH + OWN_Y_AFTER):
         ab_matmul(t)
     pe.wait_ge(sem.lw2, 16)
-    for t in range(NCH):
-        y_matmul(t)
-    for t in range(NCH, 3 * NCH):
+    y_matmul(0)
+    y_matmul(1)
+    for t in range(NCH + OWN_Y_AFTER, NT):
         ab_matmul(t)
-    for t in range(NCH, 2 * NCH):
-        y_matmul(t)
-    for t in range(3 * NCH, NT):
-        ab_matmul(t)
-    for t in range(2 * NCH, NT):
+    for t in (2, 3, 4, 6, 5, 7):
         y_matmul(t)
 
     for t in range(NT):
         act.wait_ge(done("a", t), 1)
+        act.wait_ge(done("b", t), 1)
         act.activation(col(T.s, t), bank_a(t), ActivationFunctionType.Silu).then_inc(done("s", t), 1)
 
     for t in range(NT):
         dve.wait_ge(done("s", t), 1)
         dve.wait_ge(done("b", t), 1)
         dve.tensor_tensor(col(T.h, t), col(T.s, t), bank_b(t), AluOpType.mult).then_inc(done("h", t), 1)
-    for c in range(NCH):
-        dve.wait_ge(sem["y%d" % c], 1)
-        dve.tensor_copy(col(T.o, c), bank(c)).then_inc(sem["o%d" % c], 1)
+    for p, (first, width) in enumerate(PIECES):
+        dve.wait_ge(sem["y%d" % p], 1)
+        dve.tensor_copy(T.o[:, first:first + width], bank_y(p)).then_inc(sem["o%d" % p], 1)
 
-    sync.wait_ge(sem.o0, 1)
-    sync.dma_start(col(T.y, 0), col(T.o, 0)).then_inc(sem.st0, 16)
-    act.wait_ge(sem.o1, 1)
-    act.dma_start(col(T.y, 1), col(T.o, 1)).then_inc(sem.st1, 16)
-    sync.wait_ge(sem.st0, 16)
-    act.wait_ge(sem.st1, 16)
+    for p, (first, width) in enumerate(PIECES):
+        q = act if p == 0 else sync
+        q.wait_ge(sem["o%d" % p], 1)
+        q.dma_start(T.y[:, first:first + width], T.o[:, first:first + width]).then_inc(sem["st%d" % p], 16)
+    for p in range(np_):
+        (act if p == 0 else sync).wait_ge(sem["st%d" % p], 16)

from concourse.mybir import AluOpType, ActivationFunctionType

D = 128
TK = 512
C = 256
Q = C // 2
NCH = TK // C
NR = 4
WC = 3 * D
NT = NR * NCH
NCORES = 112
PIECES = [(0, C), (C, Q), (C + Q, Q)]
NI = 8 - len(PIECES)
OWN_Y_AFTER = 3

SCRATCH = {
    "wall": ("sbuf", [D, NR * WC], "bfloat16"),
    "xs": ("sbuf", [D, TK], "bfloat16"),
    "s": ("sbuf", [D, NT * C], "float32"),
    "h": ("sbuf", [D, NT * C], "bfloat16"),
    "o": ("sbuf", [D, TK], "bfloat16"),
}
for _b in range(8):
    SCRATCH["p%d" % _b] = ("psum", [D, 512], "float32")

SEMAPHORES = (["lw1", "lw3", "lw2", "lx0", "lx1", "sent", "up1", "up2", "up3", "down1", "down2", "down3", "qdown"]
              + ["%s%d" % (q, i) for q in "absh" for i in range(NT)]
              + ["%s%d" % (q, p) for q in ("y", "o", "st") for p in range(len(PIECES))])


def _links(topo, a, b):
    ca, cb = topo.chip(a), topo.chip(b)
    if ca == cb:
        return 0
    return 1 if (topo.mates(ca, cb) or topo.same_plane(ca, cb)) else 2


def _ones(mask):
    return bin(mask).count("1")


def rank_program(g, core, T, topo):
    cores = T.cores
    n = len(cores)
    sem = T.sem

    offs = sorted(range(1, n), key=lambda k: (max(_links(topo, cores[i], cores[(i + k) % n]) for i in range(n)), k))
    k_help = offs[-1]

    def helper_of(i):
        me, dst = cores[i], cores[(i + k_help) % n]
        return [c for c in range(NCORES) if c not in cores and topo.chip(c) == topo.chip(me)
                and topo.die(c) == topo.die(me) and topo.may_write(c, dst)][0]

    def slot(j, m, m_end=None):
        return T.wall[:, j * WC + m * D:j * WC + (m + 1 if m_end is None else m_end) * D]

    def feed_mask(i):
        on = topo.mask(cores[i], helper_of(i))
        for k in offs:
            on &= ~topo.mask(cores[i], cores[(i + k) % n])
        return on

    def write(dst, ap, mask, remote_sem):
        rid, pid, _ = topo.addr(dst)
        g.remote_dma(ap, ap, remote_sem, sem.sent, pid, rid, mask)
        return _ones(mask)

    for i in range(n):
        if core == helper_of(i):
            dst = cores[(i + k_help) % n]
            g.wait_ge(sem.qdown, _ones(feed_mask(i)))
            g.wait_ge(sem.sent, write(dst, slot(i, 2), topo.mask(core, dst), sem.down3))
            return

    rank = T.rank_of(core)
    if rank is None:
        return
    pe, act, dve, sync = g.tensor, g.scalar, g.vector, g.sync

    sync.dma_start(slot(rank, 0), T.w1[:]).then_inc(sem.lw1, 16)
    act.dma_start(slot(rank, 1), T.w3[:]).then_inc(sem.lw3, 16)
    sync.dma_start(T.xs[:, 0:C], T.x[:, 0:C]).then_inc(sem.lx0, 16)
    act.dma_start(slot(rank, 2), T.w2[:]).then_inc(sem.lw2, 16)
    sync.dma_start(T.xs[:, C:TK], T.x[:, C:TK]).then_inc(sem.lx1, 16)

    dsts = [cores[(rank + k) % n] for k in offs]
    assert all(topo.may_write(core, d) for d in dsts)
    up, down = slot(rank, 0, 2), slot(rank, 2)
    g.wait_ge(sem.lw1, 16)
    g.wait_ge(sem.lw3, 16)
    left = write(dsts[0], up, topo.mask(core, dsts[0]), sem.up1)
    g.wait_ge(sem.lw2, 16)
    left += write(helper_of(rank), down, feed_mask(rank), sem.qdown)
    left += write(dsts[1], up, topo.mask(core, dsts[1]), sem.up2)
    left += write(dsts[2], up, topo.mask(core, dsts[2]), sem.up3)
    left += write(dsts[0], down, topo.mask(core, dsts[0]), sem.down1)
    left += write(dsts[1], down, topo.mask(core, dsts[1]), sem.down2)
    g.wait_ge(sem.sent, left)

    order = [rank] + [(rank - k) % n for k in offs]
    eng_up = [0] + [_ones(topo.mask(cores[j], core)) for j in order[1:]]
    eng_down = eng_up[:n - 1] + [_ones(topo.mask(helper_of(order[-1]), core))]
    np_ = len(PIECES)

    def bank_a(t):
        return T["p%d" % (np_ + t % NI)][:, 0:C]

    def bank_b(t):
        return T["p%d" % (np_ + t % NI)][:, C:2 * C]

    def bank_y(p):
        return T["p%d" % p][:, 0:PIECES[p][1]]

    def done(q, t):
        return sem["%s%d" % (q, t)]

    def col(buf, t):
        return buf[:, t * C:(t + 1) * C]

    def ab_matmul(t):
        jj, c = divmod(t, NCH)
        if c == 0 and jj > 0:
            pe.wait_ge(sem["up%d" % jj], eng_up[jj])
        if t >= NI:
            pe.wait_ge(done("s", t - NI), 1)
            pe.wait_ge(done("h", t - NI), 1)
        pe.matmul(bank_a(t), slot(order[jj], 0), col(T.xs, c), True, True).then_inc(done("a", t), 1)
        pe.matmul(bank_b(t), slot(order[jj], 1), col(T.xs, c), True, True).then_inc(done("b", t), 1)

    def y_matmul(t):
        jj, c = divmod(t, NCH)
        if c == 0 and jj > 0:
            pe.wait_ge(sem["down%d" % jj], eng_down[jj])
        pe.wait_ge(done("h", t), 1)
        for p, (first, width) in enumerate(PIECES):
            if first // C != c:
                continue
            lo = t * C + first - c * C
            mm = pe.matmul(bank_y(p), slot(order[jj], 2), T.h[:, lo:lo + width], jj == 0, jj == n - 1)
            if jj == n - 1:
                mm.then_inc(sem["y%d" % p], 1)

    pe.wait_ge(sem.lw1, 16)
    pe.wait_ge(sem.lw3, 16)
    pe.wait_ge(sem.lx0, 16)
    ab_matmul(0)
    pe.wait_ge(sem.lx1, 16)
    ab_matmul(1)
    for t in range(NCH, NCH + OWN_Y_AFTER):
        ab_matmul(t)
    pe.wait_ge(sem.lw2, 16)
    y_matmul(0)
    y_matmul(1)
    for t in range(NCH + OWN_Y_AFTER, NT):
        ab_matmul(t)
    for t in (2, 3, 4, 6, 5, 7):
        y_matmul(t)

    for t in range(NT):
        act.wait_ge(done("a", t), 1)
        act.wait_ge(done("b", t), 1)
        act.activation(col(T.s, t), bank_a(t), ActivationFunctionType.Silu).then_inc(done("s", t), 1)

    for t in range(NT):
        dve.wait_ge(done("s", t), 1)
        dve.wait_ge(done("b", t), 1)
        dve.tensor_tensor(col(T.h, t), col(T.s, t), bank_b(t), AluOpType.mult).then_inc(done("h", t), 1)
    for p, (first, width) in enumerate(PIECES):
        dve.wait_ge(sem["y%d" % p], 1)
        dve.tensor_copy(T.o[:, first:first + width], bank_y(p)).then_inc(sem["o%d" % p], 1)

    for p, (first, width) in enumerate(PIECES):
        q = act if p == 0 else sync
        q.wait_ge(sem["o%d" % p], 1)
        q.dma_start(T.y[:, first:first + width], T.o[:, first:first + width]).then_inc(sem["st%d" % p], 16)
    for p in range(np_):
        (act if p == 0 else sync).wait_ge(sem["st%d" % p], 16)
